import numpy as np, ml_dtypes
CORES = [61,69,101,62,70,102]
N = 6
TK, NT = 64, 3
def setup_inputs(rng):
    x = rng.standard_normal((NT, 128, TK), dtype=np.float32).astype(ml_dtypes.bfloat16)
    return {"x": np.broadcast_to(x, (2, NT, 128, TK)).reshape(N, 128, TK).copy(), "w": rng.standard_normal((N, 128, NT * 128), dtype=np.float32).astype(ml_dtypes.bfloat16)}
def setup_inputs_big(rng):
    d = setup_inputs(rng)
    for k in ("x", "w"): d[k] = (d[k].astype(np.float32) * 1024.0).astype(d[k].dtype)
    return d
def setup_inputs_small(rng):
    d = setup_inputs(rng)
    for k in ("x", "w"): d[k] = (d[k].astype(np.float32) * (1 / 1024.0)).astype(d[k].dtype)
    return d
def setup_inputs_apart(rng):
    d = setup_inputs(rng)
    f = (10.0 ** rng.permutation(np.linspace(-1.5, 1.5, N))).astype(np.float32).reshape(N, 1, 1)
    for k in ("x", "w"): d[k] = (d[k].astype(np.float32) * f).astype(d[k].dtype)
    return d
def tie_inputs(x):
    x = dict(x)
    x["x"] = np.concatenate([x["x"][:NT], x["x"][:NT]])
    return x
def reference(x, w):
    X, W = x.astype(np.float64), w.astype(np.float64)
    y = np.stack([sum(W[r][:, 128 * j:128 * j + 128].T @ X[j if r < NT else j + NT] for j in range(NT)) for r in range(N)])
    return {"y": y.astype(ml_dtypes.bfloat16 if x.dtype != np.float64 else np.float64)}

@@ -1,0 +1,112 @@
+from concourse.bass import DstId, RemoteDMATransfer
+
+NT = 3
+TK = 64
+KH = 2
+
+SCRATCH = {
+    "xs": ("dram", [128, TK], "bfloat16"),
+    "l0": ("dram", [128, TK], "bfloat16"),
+    "l1": ("dram", [128, TK], "bfloat16"),
+    "l2": ("dram", [128, TK], "bfloat16"),
+    "xt0": ("sbuf", [128 // KH, KH * TK], "bfloat16"),
+    "xt1": ("sbuf", [128 // KH, KH * TK], "bfloat16"),
+    "xt2": ("sbuf", [128 // KH, KH * TK], "bfloat16"),
+    "ws": ("sbuf", [128 // KH, KH * NT * 128], "bfloat16"),
+    "acc": ("psum", [128, TK], "float32"),
+    "ys": ("sbuf", [128, TK], "bfloat16"),
+}
+SEMAPHORES = ["src_ready", "go", "w_in", "own_in", "arr0", "arr1", "arr2", "in0", "in1", "in2",
+              "sent", "mm", "cast", "stored"]
+
+
+def _bits(m):
+    return [i for i in range(m.bit_length()) if (m >> i) & 1]
+
+
+def _plan(cores, topo):
+    dests = {c: [] for c in cores}
+    for j in range(NT):
+        holders = [cores[j], cores[j + NT]]
+        todo = [cores[r] for r in range(len(cores)) if r % NT != j]
+        todo.sort(key=lambda d: sum(1 for h in holders if topo.may_write(h, d)))
+        for d in todo:
+            legal = [h for h in holders if topo.may_write(h, d)]
+            dests[min(legal, key=lambda h: len(dests[h]))].append(d)
+    plan = {}
+    for s in cores:
+        plan[s] = []
+        if not dests[s]:
+            continue
+        common = topo.mask(s, dests[s][0])
+        for d in dests[s]:
+            common &= topo.mask(s, d)
+        eng = _bits(common)
+        share = 1
+        while share * 2 * len(dests[s]) <= len(eng):
+            share *= 2
+        for i, d in enumerate(dests[s]):
+            m = 0
+            for e in eng[i * share:(i + 1) * share]:
+                m |= 1 << e
+            plan[s].append((d, m, share))
+    return plan
+
+
+def rank_program(g, core, T, topo):
+    rank = T.rank_of(core)
+    if rank is None:
+        return
+    own = rank % NT
+    plan = _plan(T.cores, topo)
+
+    incoming = {}
+    for s in T.cores:
+        for d, m, n in plan[s]:
+            if d == core:
+                two_hops = 0 if topo.same_plane(topo.chip(s), topo.chip(d)) else 1
+                incoming[T.rank_of(s) % NT] = (n, (len(plan[s]), two_hops))
+    order = sorted(incoming, key=lambda j: incoming[j][1])
+
+    g.sync.dma_start(out=T.xs[:], in_=T.x[:]).then_inc(T.sem.src_ready, 16)
+    g.sync.sem_inc(T.sem.go, 1)
+    g.scalar.wait_ge(T.sem.go, 1)
+    g.scalar.dma_start(out=T["xt%d" % own][:], in_=T.x[:]).then_inc(T.sem.own_in, 16)
+    g.scalar.dma_start(out=T.ws[:], in_=T.w[:]).then_inc(T.sem.w_in, 16)
+
+    g.wait_ge(T.sem.src_ready, 16)
+    if plan[core]:
+        transfers = []
+        for d, m, n in plan[core]:
+            rid, pid, _ = topo.addr(d)
+            transfers.append(RemoteDMATransfer(dst_ids=[DstId(rid=rid, pnc=pid)], dma_engine_mask=m,
+                                               remote_sem=T.sem["arr%d" % own],
+                                               src=T.xs[:], dst=T["l%d" % own][:]))
+        g.remote_dma_fused(transfers, local_sem=T.sem.sent)
+
+    for q, j in zip((g.scalar, g.sync), order):
+        q.wait_ge(T.sem["arr%d" % j], incoming[j][0])
+        q.dma_start(out=T["xt%d" % j][:], in_=T["l%d" % j][:]).then_inc(T.sem["in%d" % j], 16)
+
+    seq = [own] + order
+    g.tensor.wait_ge(T.sem.w_in, 16)
+    g.tensor.wait_ge(T.sem.own_in, 16)
+    for t, j in enumerate(seq):
+        if j != own:
+            g.tensor.wait_ge(T.sem["in%d" % j], 16)
+        for i in range(KH):
+            c0 = i * NT * 128 + 128 * j
+            last = t == len(seq) - 1 and i == KH - 1
+            ins = g.tensor.matmul(T.acc[:], T.ws[:, c0:c0 + 128], T["xt%d" % j][:, i * TK:(i + 1) * TK],
+                                  start=(t == 0 and i == 0), stop=last)
+            if last:
+                ins.then_inc(T.sem.mm, 1)
+
+    g.vector.wait_ge(T.sem.mm, 1)
+    g.vector.tensor_copy(out=T.ys[:], in_=T.acc[:]).then_inc(T.sem.cast, 1)
+    g.sync.wait_ge(T.sem.cast, 1)
+    g.sync.dma_start(out=T.y[:], in_=T.ys[:]).then_inc(T.sem.stored, 16)
+    g.sync.wait_ge(T.sem.stored, 16)
+
+    if plan[core]:
+        g.wait_ge(T.sem.sent, sum(n for _, _, n in plan[core]))

@@ -2,17 +2,17 @@ from concourse.bass import DstId, RemoteDMATransfer
 
 NT = 3
 TK = 64
-KH = 2
+ROWS_MAX = 32
 
 SCRATCH = {
     "xs": ("dram", [128, TK], "bfloat16"),
     "l0": ("dram", [128, TK], "bfloat16"),
     "l1": ("dram", [128, TK], "bfloat16"),
     "l2": ("dram", [128, TK], "bfloat16"),
-    "xt0": ("sbuf", [128 // KH, KH * TK], "bfloat16"),
-    "xt1": ("sbuf", [128 // KH, KH * TK], "bfloat16"),
-    "xt2": ("sbuf", [128 // KH, KH * TK], "bfloat16"),
-    "ws": ("sbuf", [128 // KH, KH * NT * 128], "bfloat16"),
+    "xt0": ("sbuf", [128, TK], "bfloat16"),
+    "xt1": ("sbuf", [128, TK], "bfloat16"),
+    "xt2": ("sbuf", [128, TK], "bfloat16"),
+    "ws": ("sbuf", [128, NT * 128], "bfloat16"),
     "acc": ("psum", [128, TK], "float32"),
     "ys": ("sbuf", [128, TK], "bfloat16"),
 }
@@ -24,6 +24,19 @@ def _bits(m):
     return [i for i in range(m.bit_length()) if (m >> i) & 1]
 
 
+def _shares(eng, n):
+    share = 1
+    while share * 2 * n <= len(eng):
+        share *= 2
+    masks = []
+    for i in range(n):
+        m = 0
+        for e in eng[i * share:(i + 1) * share]:
+            m |= 1 << e
+        masks.append(m)
+    return masks, share
+
+
 def _plan(cores, topo):
     dests = {c: [] for c in cores}
     for j in range(NT):
@@ -33,24 +46,54 @@ def _plan(cores, topo):
         for d in todo:
             legal = [h for h in holders if topo.may_write(h, d)]
             dests[min(legal, key=lambda h: len(dests[h]))].append(d)
-    plan = {}
+
+    def engines(s, ds):
+        common = topo.mask(s, ds[0])
+        for d in ds:
+            common &= topo.mask(s, d)
+        return _bits(common)
+
+    calls = {c: [] for c in cores}
+    passes = {c: [] for c in cores}
+    need = {c: {} for c in cores}
     for s in cores:
-        plan[s] = []
         if not dests[s]:
             continue
-        common = topo.mask(s, dests[s][0])
+        j = cores.index(s) % NT
+        eng = engines(s, dests[s])
+        masks, share = _shares(eng, len(dests[s]))
+        if 128 // share <= ROWS_MAX:
+            calls[s].append([(d, m, share, True) for d, m in zip(dests[s], masks)])
+            for d in dests[s]:
+                need[d][j] = (share, 0)
+            continue
+        groups = {}
         for d in dests[s]:
-            common &= topo.mask(s, d)
-        eng = _bits(common)
-        share = 1
-        while share * 2 * len(dests[s]) <= len(eng):
-            share *= 2
-        for i, d in enumerate(dests[s]):
-            m = 0
-            for e in eng[i * share:(i + 1) * share]:
-                m |= 1 << e
-            plan[s].append((d, m, share))
-    return plan
+            groups.setdefault(topo.chip(d), []).append(d)
+        heads, alone = [], []
+        for ch in sorted(groups):
+            mem = sorted(groups[ch], key=lambda d: 0 if dests[d] else 1)
+            if len(mem) > 1 and dests[mem[0]]:
+                heads.append((mem[0], mem[1:]))
+            else:
+                alone += mem
+        if heads:
+            masks, share = _shares(eng, len(heads))
+            calls[s].append([(h, m, share, False) for (h, _), m in zip(heads, masks)])
+            for h, rest in heads:
+                hm = 0
+                for e in engines(h, dests[h]):
+                    hm |= 1 << e
+                for d in rest:
+                    pm = hm & topo.mask(h, d)
+                    passes[h].append((j, share, d, pm))
+                    need[d][j] = (len(_bits(pm)), 2)
+        direct = [h for h, _ in heads] + alone
+        masks, share = _shares(eng, len(direct))
+        calls[s].append([(d, m, share, True) for d, m in zip(direct, masks)])
+        for d in direct:
+            need[d][j] = (share, 1)
+    return calls, passes, need
 
 
 def rank_program(g, core, T, topo):
@@ -58,49 +101,45 @@ def rank_program(g, core, T, topo):
     if rank is None:
         return
     own = rank % NT
-    plan = _plan(T.cores, topo)
+    calls, passes, need = _plan(T.cores, topo)
+    order = sorted(need[core], key=lambda j: need[core][j][1])
 
-    incoming = {}
-    for s in T.cores:
-        for d, m, n in plan[s]:
-            if d == core:
-                two_hops = 0 if topo.same_plane(topo.chip(s), topo.chip(d)) else 1
-                incoming[T.rank_of(s) % NT] = (n, (len(plan[s]), two_hops))
-    order = sorted(incoming, key=lambda j: incoming[j][1])
-
-    g.sync.dma_start(out=T.xs[:], in_=T.x[:]).then_inc(T.sem.src_ready, 16)
+    if calls[core]:
+        g.sync.dma_start(out=T.xs[:], in_=T.x[:]).then_inc(T.sem.src_ready, 16)
     g.sync.sem_inc(T.sem.go, 1)
     g.scalar.wait_ge(T.sem.go, 1)
     g.scalar.dma_start(out=T["xt%d" % own][:], in_=T.x[:]).then_inc(T.sem.own_in, 16)
     g.scalar.dma_start(out=T.ws[:], in_=T.w[:]).then_inc(T.sem.w_in, 16)
 
-    g.wait_ge(T.sem.src_ready, 16)
-    if plan[core]:
+    left = 0
+    if calls[core]:
+        g.wait_ge(T.sem.src_ready, 16)
+    for call in calls[core]:
         transfers = []
-        for d, m, n in plan[core]:
+        for d, m, n, sbuf in call:
             rid, pid, _ = topo.addr(d)
             transfers.append(RemoteDMATransfer(dst_ids=[DstId(rid=rid, pnc=pid)], dma_engine_mask=m,
-                                               remote_sem=T.sem["arr%d" % own],
-                                               src=T.xs[:], dst=T["l%d" % own][:]))
+                                               remote_sem=T.sem[("in%d" if sbuf else "arr%d") % own],
+                                               src=T.xs[:], dst=T[("xt%d" if sbuf else "l%d") % own][:]))
+            left += n
         g.remote_dma_fused(transfers, local_sem=T.sem.sent)
 
-    for q, j in zip((g.scalar, g.sync), order):
-        q.wait_ge(T.sem["arr%d" % j], incoming[j][0])
-        q.dma_start(out=T["xt%d" % j][:], in_=T["l%d" % j][:]).then_inc(T.sem["in%d" % j], 16)
+    for j, n, d, pm in passes[core]:
+        g.wait_ge(T.sem["arr%d" % j], n)
+        rid, pid, _ = topo.addr(d)
+        g.remote_dma(T["xt%d" % j][:], T["l%d" % j][:], T.sem["in%d" % j], T.sem.sent, pid, rid, pm)
+        left += len(_bits(pm))
 
     seq = [own] + order
     g.tensor.wait_ge(T.sem.w_in, 16)
     g.tensor.wait_ge(T.sem.own_in, 16)
     for t, j in enumerate(seq):
         if j != own:
-            g.tensor.wait_ge(T.sem["in%d" % j], 16)
-        for i in range(KH):
-            c0 = i * NT * 128 + 128 * j
-            last = t == len(seq) - 1 and i == KH - 1
-            ins = g.tensor.matmul(T.acc[:], T.ws[:, c0:c0 + 128], T["xt%d" % j][:, i * TK:(i + 1) * TK],
-                                  start=(t == 0 and i == 0), stop=last)
-            if last:
-                ins.then_inc(T.sem.mm, 1)
+            g.tensor.wait_ge(T.sem["in%d" % j], need[core][j][0])
+        last = t == len(seq) - 1
+        ins = g.tensor.matmul(T.acc[:], T.ws[:, 128 * j:128 * j + 128], T["xt%d" % j][:], start=(t == 0), stop=last)
+        if last:
+            ins.then_inc(T.sem.mm, 1)
 
     g.vector.wait_ge(T.sem.mm, 1)
     g.vector.tensor_copy(out=T.ys[:], in_=T.acc[:]).then_inc(T.sem.cast, 1)
@@ -108,5 +147,5 @@ def rank_program(g, core, T, topo):
     g.sync.dma_start(out=T.y[:], in_=T.ys[:]).then_inc(T.sem.stored, 16)
     g.sync.wait_ge(T.sem.stored, 16)
 
-    if plan[core]:
-        g.wait_ge(T.sem.sent, sum(n for _, _, n in plan[core]))
+    if left:
+        g.wait_ge(T.sem.sent, left)

from concourse.bass import DstId, RemoteDMATransfer

NT = 3
TK = 64
ROWS_MAX = 32

SCRATCH = {
    "xs": ("dram", [128, TK], "bfloat16"),
    "l0": ("dram", [128, TK], "bfloat16"),
    "l1": ("dram", [128, TK], "bfloat16"),
    "l2": ("dram", [128, TK], "bfloat16"),
    "xt0": ("sbuf", [128, TK], "bfloat16"),
    "xt1": ("sbuf", [128, TK], "bfloat16"),
    "xt2": ("sbuf", [128, TK], "bfloat16"),
    "ws": ("sbuf", [128, NT * 128], "bfloat16"),
    "acc": ("psum", [128, TK], "float32"),
    "ys": ("sbuf", [128, TK], "bfloat16"),
}
SEMAPHORES = ["src_ready", "go", "w_in", "own_in", "arr0", "arr1", "arr2", "in0", "in1", "in2",
              "sent", "mm", "cast", "stored"]


def _bits(m):
    return [i for i in range(m.bit_length()) if (m >> i) & 1]


def _shares(eng, n):
    share = 1
    while share * 2 * n <= len(eng):
        share *= 2
    masks = []
    for i in range(n):
        m = 0
        for e in eng[i * share:(i + 1) * share]:
            m |= 1 << e
        masks.append(m)
    return masks, share


def _plan(cores, topo):
    dests = {c: [] for c in cores}
    for j in range(NT):
        holders = [cores[j], cores[j + NT]]
        todo = [cores[r] for r in range(len(cores)) if r % NT != j]
        todo.sort(key=lambda d: sum(1 for h in holders if topo.may_write(h, d)))
        for d in todo:
            legal = [h for h in holders if topo.may_write(h, d)]
            dests[min(legal, key=lambda h: len(dests[h]))].append(d)

    def engines(s, ds):
        common = topo.mask(s, ds[0])
        for d in ds:
            common &= topo.mask(s, d)
        return _bits(common)

    calls = {c: [] for c in cores}
    passes = {c: [] for c in cores}
    need = {c: {} for c in cores}
    for s in cores:
        if not dests[s]:
            continue
        j = cores.index(s) % NT
        eng = engines(s, dests[s])
        masks, share = _shares(eng, len(dests[s]))
        if 128 // share <= ROWS_MAX:
            calls[s].append([(d, m, share, True) for d, m in zip(dests[s], masks)])
            for d in dests[s]:
                need[d][j] = (share, 0)
            continue
        groups = {}
        for d in dests[s]:
            groups.setdefault(topo.chip(d), []).append(d)
        heads, alone = [], []
        for ch in sorted(groups):
            mem = sorted(groups[ch], key=lambda d: 0 if dests[d] else 1)
            if len(mem) > 1 and dests[mem[0]]:
                heads.append((mem[0], mem[1:]))
            else:
                alone += mem
        if heads:
            masks, share = _shares(eng, len(heads))
            calls[s].append([(h, m, share, False) for (h, _), m in zip(heads, masks)])
            for h, rest in heads:
                hm = 0
                for e in engines(h, dests[h]):
                    hm |= 1 << e
                for d in rest:
                    pm = hm & topo.mask(h, d)
                    passes[h].append((j, share, d, pm))
                    need[d][j] = (len(_bits(pm)), 2)
        direct = [h for h, _ in heads] + alone
        masks, share = _shares(eng, len(direct))
        calls[s].append([(d, m, share, True) for d, m in zip(direct, masks)])
        for d in direct:
            need[d][j] = (share, 1)
    return calls, passes, need


def rank_program(g, core, T, topo):
    rank = T.rank_of(core)
    if rank is None:
        return
    own = rank % NT
    calls, passes, need = _plan(T.cores, topo)
    order = sorted(need[core], key=lambda j: need[core][j][1])

    if calls[core]:
        g.sync.dma_start(out=T.xs[:], in_=T.x[:]).then_inc(T.sem.src_ready, 16)
    g.sync.sem_inc(T.sem.go, 1)
    g.scalar.wait_ge(T.sem.go, 1)
    g.scalar.dma_start(out=T["xt%d" % own][:], in_=T.x[:]).then_inc(T.sem.own_in, 16)
    g.scalar.dma_start(out=T.ws[:], in_=T.w[:]).then_inc(T.sem.w_in, 16)

    left = 0
    if calls[core]:
        g.wait_ge(T.sem.src_ready, 16)
    for call in calls[core]:
        transfers = []
        for d, m, n, sbuf in call:
            rid, pid, _ = topo.addr(d)
            transfers.append(RemoteDMATransfer(dst_ids=[DstId(rid=rid, pnc=pid)], dma_engine_mask=m,
                                               remote_sem=T.sem[("in%d" if sbuf else "arr%d") % own],
                                               src=T.xs[:], dst=T[("xt%d" if sbuf else "l%d") % own][:]))
            left += n
        g.remote_dma_fused(transfers, local_sem=T.sem.sent)

    for j, n, d, pm in passes[core]:
        g.wait_ge(T.sem["arr%d" % j], n)
        rid, pid, _ = topo.addr(d)
        g.remote_dma(T["xt%d" % j][:], T["l%d" % j][:], T.sem["in%d" % j], T.sem.sent, pid, rid, pm)
        left += len(_bits(pm))

    seq = [own] + order
    g.tensor.wait_ge(T.sem.w_in, 16)
    g.tensor.wait_ge(T.sem.own_in, 16)
    for t, j in enumerate(seq):
        if j != own:
            g.tensor.wait_ge(T.sem["in%d" % j], need[core][j][0])
        last = t == len(seq) - 1
        ins = g.tensor.matmul(T.acc[:], T.ws[:, 128 * j:128 * j + 128], T["xt%d" % j][:], start=(t == 0), stop=last)
        if last:
            ins.then_inc(T.sem.mm, 1)

    g.vector.wait_ge(T.sem.mm, 1)
    g.vector.tensor_copy(out=T.ys[:], in_=T.acc[:]).then_inc(T.sem.cast, 1)
    g.sync.wait_ge(T.sem.cast, 1)
    g.sync.dma_start(out=T.y[:], in_=T.ys[:]).then_inc(T.sem.stored, 16)
    g.sync.wait_ge(T.sem.stored, 16)

    if left:
        g.wait_ge(T.sem.sent, left)
